import numpy as np, ml_dtypes
CORES = [10,34,74,98]
N = 4
import mx_ref
NC, G = 128, 4
C, C2 = np.float32(0.019), np.float32(0.0095)
BF = ml_dtypes.bfloat16
def cut(t, i, w=512):
    return t[:, w * i:w * i + w]
def tile(rs):
    return np.stack(rs, axis=2).reshape(128, -1).astype(BF)
def layer(w, X):
    out = []
    for i in range(G):
        for t in range(len(X)):
            p = mx_ref.matmul(mx_ref.quantize(cut(w, len(X) * i + t)), X[t])
            z = p if t == 0 else z + p
        out.append(z)
    return out
def act(Z):
    return [np.maximum(z, 0) * C for z in Z]
def act2(Z):
    return [np.maximum(z, 0) * C2 for z in Z]
def setup_inputs(rng):
    def f(*shape):
        return mx_ref.flush((rng.standard_normal(shape, dtype=np.float32) * np.exp2(rng.integers(-2, 3, shape[:-1] + (1,)))).astype(BF))
    return {"x": f(N, 128, 4 * NC), "w1": f(N, 128, G * 512), "w2": f(N, 128, G * 512), "w3": f(N, 128, G * 512)}
def setup_inputs_blocks(rng):
    d = setup_inputs(rng)
    for k in ("x", "w1", "w2", "w3"): d[k] = mx_ref.spread(d[k], rng, 2)
    return d
def setup_inputs_wide(rng):
    d = setup_inputs(rng)
    for k in ("x", "w1", "w2", "w3"): d[k] = mx_ref.flush((d[k].astype(np.float32) * np.exp2(rng.integers(-4, 5, (N, 1, 1))).astype(np.float32)).astype(BF))
    return d
def reference(x, w1, w2, w3, own=None):
    X = [mx_ref.quantize(x[j]) for j in range(N)]
    t = np.stack([np.stack([tile(act(layer(w1[r], [X[c]]))) for c in range(N)]) for r in range(N)])
    uset = t if own is None else own["t"]
    h = np.zeros((N, 128, 4 * NC), BF)
    for c in range(N):
        for r in range(N):
            P = layer(w2[r], [mx_ref.quantize(uset[r][c])])
            Z = P if r == 0 else [z + p for z, p in zip(Z, P)]
        h[c] = tile(act2(Z))
    use = h if own is None else own["h"]
    H = [mx_ref.quantize(use[j]) for j in range(N)]
    y = np.zeros((N, 128, N * G * NC), np.float32)
    for r in range(N):
        for j in range(N):
            Z = layer(w3[r], [H[j]])
            for i in range(G):
                y[r][:, NC * (G * j + i):NC * (G * j + i) + NC] = Z[i]
    return {"t": t, "h": h, "y": y}

@@ -1,0 +1,269 @@
+from concourse.mybir import dt, AluOpType, ActivationFunctionType
+
+U8 = dt.uint8
+C1, C2 = 0.019, 0.0095
+SIM_CORES = 112
+NC = 128
+SPLIT = 384
+
+_B, _F, _Q, _S8 = "bfloat16", "float32", "float8_e4m3fn_x4", "uint8"
+SCRATCH = {"ps": ("psum", [128, 4096], _F)}
+SCRATCH["xb"] = ("sbuf", [128, 512], _B)
+for _k in ("w1", "w2", "w3"):
+    SCRATCH[_k + "b"] = ("sbuf", [128, 2048], _B)
+    SCRATCH[_k + "q"] = ("sbuf", [128, 512], _Q)
+    SCRATCH[_k + "s"] = ("sbuf", [128, 512], _S8)
+SCRATCH["rw2q"] = ("sbuf", [128, 512], _Q)
+SCRATCH["rw2s"] = ("sbuf", [128, 512], _S8)
+for _k in ("x", "h"):
+    for _p in ("O", "A", "B", "S"):
+        SCRATCH[_k + "q" + _p] = ("sbuf", [128, NC], _Q)
+        SCRATCH[_k + "s" + _p] = ("sbuf", [128, NC], _S8)
+for _p in ("O", "A", "B", "S"):
+    SCRATCH["t" + _p] = ("sbuf", [128, 512], _B)
+    SCRATCH["tq" + _p] = ("sbuf", [128, NC], _Q)
+    SCRATCH["ts" + _p] = ("sbuf", [128, NC], _S8)
+    SCRATCH["y" + _p] = ("sbuf", [128, 512], _F)
+SCRATCH["rtq"] = ("sbuf", [128, NC], _Q)
+SCRATCH["rts"] = ("sbuf", [128, NC], _S8)
+for _k in ("pA", "pS", "lA", "lS", "acc", "sm"):
+    SCRATCH[_k] = ("sbuf", [128, 512], _F)
+SCRATCH["hb"] = ("sbuf", [128, 512], _B)
+
+SEMAPHORES = ["lx", "lw1", "lw2", "lw3", "qx", "qw1", "qw2", "qw3", "xloc", "w2loc", "ploc", "hloc", "outs",
+              "w2p", "w2c0", "w2c1", "rw2", "rt", "inA", "inS0", "inS1", "cpA", "cpS0", "cpS1", "acc", "th", "qh", "fwd"]
+SEMAPHORES += ["%s%d" % (_k, _r) for _k in "xh" for _r in range(4)]
+SEMAPHORES += ["t" + _p for _p in "OABS"] + ["qt" + _p for _p in "OABS"]
+SEMAPHORES += ["z%s%d" % (_p, _b) for _p in "OABS" for _b in range(4)]
+SEMAPHORES += ["u%s%d" % (_p, _b) for _p in "OAS" for _b in range(4)]
+SEMAPHORES += ["v%s%d" % (_p, _b) for _p in "OABS" for _b in range(4)]
+SEMAPHORES += ["yv" + _p for _p in "OABS"] + ["ys" + _p for _p in "OABS"]
+SEMAPHORES += ["sm%d" % _b for _b in range(4)]
+
+
+def relations(T, topo, r):
+    n = len(T.cores)
+    ch = [topo.chip(c) for c in T.cores]
+    planes = []
+    for i in range(n):
+        for p in planes:
+            if topo.same_plane(ch[i], ch[p[0]]):
+                p.append(i)
+                break
+        else:
+            planes.append([i])
+    mine, other = (planes[0], planes[1]) if r in planes[0] else (planes[1], planes[0])
+    k = mine.index(r)
+    return {"S": mine[1 - k], "B": other[k], "A": other[1 - k]}
+
+
+def helper_of(T, topo, r):
+    me = T.cores[r]
+    for c in range(SIM_CORES):
+        if topo.chip(c) == topo.chip(me) and topo.die(c) != topo.die(me) and all(topo.may_write(c, d) for d in T.cores):
+            return c
+    return None
+
+
+def rank_program(g, core, T, topo):
+    sem = T.sem
+
+    def bits(m):
+        return bin(m).count("1")
+
+    def send(dst, out, in_, rsem, lsem, mask):
+        rid, pid, _ = topo.addr(dst)
+        g.remote_dma(out, in_, sem[rsem], sem[lsem], pid, rid, mask)
+
+    def u8(name, a, b):
+        return T[name][:, a:b].bitcast(U8)
+
+    def masks(r):
+        far = topo.mask(T.cores[r], T.cores[relations(T, topo, r)["A"]])
+        return far, topo.mask(T.cores[r], helper_of(T, topo, r)) & ~far
+
+    rank = T.rank_of(core)
+    if rank is None:
+        for r in range(len(T.cores)):
+            if helper_of(T, topo, r) == core:
+                dst = T.cores[relations(T, topo, r)["B"]]
+                m = topo.mask(core, dst)
+                nn = bits(masks(r)[1])
+                g.wait_ge(sem["w2p"], nn)
+                send(dst, T.rw2s[:, :], T.rw2s[:, :], "rw2", "fwd", m)
+                g.wait_ge(sem["w2c0"], nn)
+                send(dst, u8("rw2q", 0, 256), u8("rw2q", 0, 256), "rw2", "fwd", m)
+                g.wait_ge(sem["w2c1"], nn)
+                send(dst, u8("rw2q", 256, 512), u8("rw2q", 256, 512), "rw2", "fwd", m)
+                g.wait_ge(sem["fwd"], 3 * bits(m))
+        return
+
+    rel = relations(T, topo, rank)
+    who = dict(rel)
+    who["O"] = rank
+    dst = {p: T.cores[rel[p]] for p in "ABS"}
+    hlp = helper_of(T, topo, rank)
+    far, near = masks(rank)
+    nf = bits(far)
+    te, ve, sc, sy = g.tensor, g.vector, g.scalar, g.sync
+
+    sy.dma_start(T.xb[:], T.x[:]).then_inc(sem["lx"], 16)
+    sy.wait_ge(sem["lx"], 16)
+    sy.dma_start(T.w2b[:], T.w2[:]).then_inc(sem["lw2"], 16)
+    sy.dma_start(T.w1b[:], T.w1[:]).then_inc(sem["lw1"], 16)
+    sy.wait_ge(sem["lw1"], 16)
+    sy.dma_start(T.w3b[:], T.w3[:]).then_inc(sem["lw3"], 16)
+
+    def bcast(kind, lsem):
+        rsem = "%s%d" % (kind, rank)
+        for p in "ABS":
+            send(dst[p], T[kind + "s" + p][:, :], T[kind + "sO"][:, :], rsem, lsem, far)
+            send(dst[p], u8(kind + "q" + p, 0, NC), u8(kind + "qO", 0, NC), rsem, lsem, far)
+
+    g.wait_ge(sem["qx"], 1)
+    bcast("x", "xloc")
+    g.wait_ge(sem["qw2"], 1)
+    send(hlp, T.rw2s[:, :], T.w2s[:, :], "w2p", "w2loc", near)
+    send(hlp, u8("rw2q", 0, 256), u8("w2q", 0, 256), "w2c0", "w2loc", near)
+    send(hlp, u8("rw2q", 256, 512), u8("w2q", 256, 512), "w2c1", "w2loc", near)
+    g.wait_ge(sem["cpA"], 4)
+    send(dst["A"], T.lA[:, :], T.pA[:, :], "inA", "ploc", far)
+    g.wait_ge(sem["qtB"], 1)
+    send(dst["B"], u8("rtq", 0, NC), u8("tqB", 0, NC), "rt", "ploc", far)
+    send(dst["B"], T.rts[:, :], T.tsB[:, :], "rt", "ploc", far)
+    g.wait_ge(sem["cpS0"], 3)
+    send(dst["S"], T.lS[:, 0:SPLIT], T.pS[:, 0:SPLIT], "inS0", "ploc", far)
+    g.wait_ge(sem["cpS1"], 1)
+    send(dst["S"], T.lS[:, SPLIT:512], T.pS[:, SPLIT:512], "inS1", "ploc", far)
+    g.wait_ge(sem["qh"], 1)
+    bcast("h", "hloc")
+    g.wait_ge(sem["w2loc"], 3 * bits(near))
+
+    def mm(bank, w, wi, xq, xs, start, stop, done=None):
+        c = te.matmul_mx(T.ps[:, 512 * bank:512 * bank + NC], T[w + "q"][:, NC * wi:NC * wi + NC], T[w + "s"][:, NC * wi:NC * wi + NC],
+                         T[xq][:, :], T[xs][:, :], start, stop)
+        if done is not None:
+            c.then_inc(sem[done], 1)
+
+    def four(base, w, xq, xs, name):
+        for b in range(4):
+            mm(base + b, w, b, xq, xs, True, True, "%s%d" % (name, b))
+
+    te.wait_ge(sem["qx"], 1)
+    te.wait_ge(sem["qw1"], 1)
+    four(0, "w1", "xqO", "xsO", "zO")
+    te.wait_ge(sem["x%d" % rel["A"]], 2 * nf)
+    four(4, "w1", "xqA", "xsA", "zA")
+    te.wait_ge(sem["qw2"], 1)
+    te.wait_ge(sem["qtO"], 1)
+    te.wait_ge(sem["qtA"], 1)
+    four(0, "w2", "tqA", "tsA", "uA")
+    te.wait_ge(sem["x%d" % rel["B"]], 2 * nf)
+    four(4, "w1", "xqB", "xsB", "zB")
+    te.wait_ge(sem["x%d" % rel["S"]], 2 * nf)
+    te.wait_ge(sem["cpA"], 4)
+    four(0, "w1", "xqS", "xsS", "zS")
+    te.wait_ge(sem["qtB"], 1)
+    te.wait_ge(sem["qtS"], 1)
+    four(4, "w2", "tqS", "tsS", "uS")
+    for b in range(4):
+        mm(b, "w2", b, "tqO", "tsO", True, False)
+    te.wait_ge(sem["rw2"], 3 * nf)
+    te.wait_ge(sem["rt"], 2 * nf)
+    for b in range(4):
+        mm(b, "rw2", b, "rtq", "rts", False, True, "uO%d" % b)
+    te.wait_ge(sem["qw3"], 1)
+    te.wait_ge(sem["cpS0"], 3)
+    te.wait_ge(sem["cpS1"], 1)
+    te.wait_ge(sem["qh"], 1)
+    four(4, "w3", "hqO", "hsO", "vO")
+    te.wait_ge(sem["h%d" % rel["A"]], 2 * nf)
+    four(0, "w3", "hqA", "hsA", "vA")
+    te.wait_ge(sem["h%d" % rel["B"]], 2 * nf)
+    te.wait_ge(sem["yvO"], 2)
+    te.wait_ge(sem["ysO"], 2)
+    four(4, "w3", "hqB", "hsB", "vB")
+    te.wait_ge(sem["h%d" % rel["S"]], 2 * nf)
+    te.wait_ge(sem["yvA"], 2)
+    te.wait_ge(sem["ysA"], 2)
+    four(0, "w3", "hqS", "hsS", "vS")
+
+    def psb(base, b):
+        return T.ps[:, 512 * (base + b):512 * (base + b) + NC]
+
+    def act(p, base):
+        for b in range(4):
+            if b % 2 == 0:
+                ve.wait_ge(sem["z%s%d" % (p, b)], 1)
+                ve.tensor_scalar(T["t" + p][:, b:512:4], psb(base, b), 0.0, C1, AluOpType.max, AluOpType.mult).then_inc(sem["t" + p], 1)
+            else:
+                sc.wait_ge(sem["z%s%d" % (p, b)], 1)
+                sc.activation(T["t" + p][:, b:512:4], psb(base, b), ActivationFunctionType.Relu, scale=C1).then_inc(sem["t" + p], 1)
+        ve.wait_ge(sem["t" + p], 4)
+        ve.quantize_mx(T["tq" + p][:, :], T["ts" + p][:, :], T["t" + p][:, :]).then_inc(sem["qt" + p], 1)
+
+    def copy_out(p, base):
+        for b in range(4):
+            done = "cpA" if p == "A" else ("cpS0" if NC * b < SPLIT else "cpS1")
+            o = T["p" + p][:, NC * b:NC * b + NC]
+            if b % 2 == 0:
+                ve.wait_ge(sem["u%s%d" % (p, b)], 1)
+                ve.tensor_copy(o, psb(base, b)).then_inc(sem[done], 1)
+            else:
+                sc.wait_ge(sem["u%s%d" % (p, b)], 1)
+                sc.activation(o, psb(base, b), ActivationFunctionType.Copy).then_inc(sem[done], 1)
+
+    ve.wait_ge(sem["lx"], 16)
+    ve.quantize_mx(T.xqO[:, :], T.xsO[:, :], T.xb[:, :]).then_inc(sem["qx"], 1)
+    ve.wait_ge(sem["lw2"], 16)
+    ve.quantize_mx(T.w2q[:, :], T.w2s[:, :], T.w2b[:, :]).then_inc(sem["qw2"], 1)
+    ve.wait_ge(sem["lw1"], 16)
+    ve.quantize_mx(T.w1q[:, :], T.w1s[:, :], T.w1b[:, :]).then_inc(sem["qw1"], 1)
+    act("O", 0)
+    act("A", 4)
+    copy_out("A", 0)
+    act("B", 4)
+    act("S", 0)
+    copy_out("S", 4)
+    ve.wait_ge(sem["lw3"], 16)
+    ve.quantize_mx(T.w3q[:, :], T.w3s[:, :], T.w3b[:, :]).then_inc(sem["qw3"], 1)
+
+    ve.wait_ge(sem["inA"], nf)
+    for b in range(4):
+        ve.wait_ge(sem["uO%d" % b], 1)
+        ve.tensor_tensor(T.acc[:, NC * b:NC * b + NC], psb(0, b), T.lA[:, NC * b:NC * b + NC], AluOpType.add).then_inc(sem["acc"], 1)
+    ve.wait_ge(sem["acc"], 4)
+    ve.wait_ge(sem["inS0"], nf)
+    for b in range(4):
+        if NC * b == SPLIT:
+            ve.wait_ge(sem["inS1"], nf)
+        ve.tensor_tensor(T.sm[:, NC * b:NC * b + NC], T.acc[:, NC * b:NC * b + NC], T.lS[:, NC * b:NC * b + NC], AluOpType.add).then_inc(sem["sm%d" % b], 1)
+        sc.wait_ge(sem["sm%d" % b], 1)
+        sc.activation(T.hb[:, b:512:4], T.sm[:, NC * b:NC * b + NC], ActivationFunctionType.Relu, scale=C2).then_inc(sem["th"], 1)
+    ve.wait_ge(sem["th"], 4)
+    ve.quantize_mx(T.hqO[:, :], T.hsO[:, :], T.hb[:, :]).then_inc(sem["qh"], 1)
+
+    for p, base in (("O", 4), ("A", 0), ("B", 4), ("S", 0)):
+        for b in (0, 1):
+            ve.wait_ge(sem["v%s%d" % (p, b)], 1)
+            ve.tensor_copy(T["y" + p][:, NC * b:NC * b + NC], psb(base, b)).then_inc(sem["yv" + p], 1)
+        for b in (2, 3):
+            sc.wait_ge(sem["v%s%d" % (p, b)], 1)
+            sc.activation(T["y" + p][:, NC * b:NC * b + NC], psb(base, b), ActivationFunctionType.Copy).then_inc(sem["ys" + p], 1)
+
+    sy.wait_ge(sem["qtO"], 1)
+    sy.dma_start(T.t[who["O"]], T.tO[:, :]).then_inc(sem["outs"], 16)
+    sy.wait_ge(sem["xloc"], 6 * nf)
+    sy.wait_ge(sem["ploc"], 5 * nf)
+    for p in "ABS":
+        sy.wait_ge(sem["qt" + p], 1)
+        sy.dma_start(T.t[who[p]], T["t" + p][:, :]).then_inc(sem["outs"], 16)
+    sy.wait_ge(sem["th"], 4)
+    sy.dma_start(T.h[:], T.hb[:, :]).then_inc(sem["outs"], 16)
+    for p in "OABS":
+        c0 = 512 * who[p]
+        sy.wait_ge(sem["yv" + p], 2)
+        sy.wait_ge(sem["ys" + p], 2)
+        sy.dma_start(T.y[:, c0:c0 + 512], T["y" + p][:, :]).then_inc(sem["outs"], 16)
+    sy.wait_ge(sem["hloc"], 6 * nf)
+    sy.wait_ge(sem["outs"], 16 * 9)

@@ -5,6 +5,8 @@ C1, C2 = 0.019, 0.0095
 SIM_CORES = 112
 NC = 128
 SPLIT = 384
+VIA = 2
+HALF = 256
 
 _B, _F, _Q, _S8 = "bfloat16", "float32", "float8_e4m3fn_x4", "uint8"
 SCRATCH = {"ps": ("psum", [128, 4096], _F)}
@@ -28,10 +30,12 @@ SCRATCH["rtq"] = ("sbuf", [128, NC], _Q)
 SCRATCH["rts"] = ("sbuf", [128, NC], _S8)
 for _k in ("pA", "pS", "lA", "lS", "acc", "sm"):
     SCRATCH[_k] = ("sbuf", [128, 512], _F)
+SCRATCH["rp"] = ("sbuf", [128, NC * VIA], _F)
 SCRATCH["hb"] = ("sbuf", [128, 512], _B)
 
 SEMAPHORES = ["lx", "lw1", "lw2", "lw3", "qx", "qw1", "qw2", "qw3", "xloc", "w2loc", "ploc", "hloc", "outs",
-              "w2p", "w2c0", "w2c1", "rw2", "rt", "inA", "inS0", "inS1", "cpA", "cpS0", "cpS1", "acc", "th", "qh", "fwd"]
+              "w2p", "w2c", "rp", "rw2", "rt", "inA0", "inA1", "inS0", "inS1", "cpA0", "cpA1", "cpS0", "cpS1",
+              "acc", "th", "qh", "fwd"]
 SEMAPHORES += ["%s%d" % (_k, _r) for _k in "xh" for _r in range(4)]
 SEMAPHORES += ["t" + _p for _p in "OABS"] + ["qt" + _p for _p in "OABS"]
 SEMAPHORES += ["z%s%d" % (_p, _b) for _p in "OABS" for _b in range(4)]
@@ -82,19 +86,21 @@ def rank_program(g, core, T, topo):
         far = topo.mask(T.cores[r], T.cores[relations(T, topo, r)["A"]])
         return far, topo.mask(T.cores[r], helper_of(T, topo, r)) & ~far
 
+    kv = NC * VIA
     rank = T.rank_of(core)
     if rank is None:
         for r in range(len(T.cores)):
             if helper_of(T, topo, r) == core:
-                dst = T.cores[relations(T, topo, r)["B"]]
-                m = topo.mask(core, dst)
+                rel = relations(T, topo, r)
+                to_a, to_b = T.cores[rel["A"]], T.cores[rel["B"]]
+                m = topo.mask(core, to_b)
                 nn = bits(masks(r)[1])
                 g.wait_ge(sem["w2p"], nn)
-                send(dst, T.rw2s[:, :], T.rw2s[:, :], "rw2", "fwd", m)
-                g.wait_ge(sem["w2c0"], nn)
-                send(dst, u8("rw2q", 0, 256), u8("rw2q", 0, 256), "rw2", "fwd", m)
-                g.wait_ge(sem["w2c1"], nn)
-                send(dst, u8("rw2q", 256, 512), u8("rw2q", 256, 512), "rw2", "fwd", m)
+                send(to_b, T.rw2s[:, :], T.rw2s[:, :], "rw2", "fwd", m)
+                g.wait_ge(sem["w2c"], nn)
+                send(to_b, u8("rw2q", 0, HALF), u8("rw2q", 0, HALF), "rw2", "fwd", m)
+                g.wait_ge(sem["rp"], nn)
+                send(to_a, T.lA[:, 0:kv], T.rp[:, :], "inA0", "fwd", m)
                 g.wait_ge(sem["fwd"], 3 * bits(m))
         return
 
@@ -108,10 +114,10 @@ def rank_program(g, core, T, topo):
     te, ve, sc, sy = g.tensor, g.vector, g.scalar, g.sync
 
     sy.dma_start(T.xb[:], T.x[:]).then_inc(sem["lx"], 16)
+    sy.dma_start(T.w1b[:], T.w1[:]).then_inc(sem["lw1"], 16)
     sy.wait_ge(sem["lx"], 16)
     sy.dma_start(T.w2b[:], T.w2[:]).then_inc(sem["lw2"], 16)
-    sy.dma_start(T.w1b[:], T.w1[:]).then_inc(sem["lw1"], 16)
-    sy.wait_ge(sem["lw1"], 16)
+    sy.wait_ge(sem["qtA"], 1)
     sy.dma_start(T.w3b[:], T.w3[:]).then_inc(sem["lw3"], 16)
 
     def bcast(kind, lsem):
@@ -124,10 +130,12 @@ def rank_program(g, core, T, topo):
     bcast("x", "xloc")
     g.wait_ge(sem["qw2"], 1)
     send(hlp, T.rw2s[:, :], T.w2s[:, :], "w2p", "w2loc", near)
-    send(hlp, u8("rw2q", 0, 256), u8("w2q", 0, 256), "w2c0", "w2loc", near)
-    send(hlp, u8("rw2q", 256, 512), u8("w2q", 256, 512), "w2c1", "w2loc", near)
-    g.wait_ge(sem["cpA"], 4)
-    send(dst["A"], T.lA[:, :], T.pA[:, :], "inA", "ploc", far)
+    send(hlp, u8("rw2q", 0, HALF), u8("w2q", 0, HALF), "w2c", "w2loc", near)
+    send(dst["B"], u8("rw2q", HALF, 512), u8("w2q", HALF, 512), "rw2", "w2loc", far)
+    g.wait_ge(sem["cpA0"], VIA)
+    send(hlp, T.rp[:, :], T.pA[:, 0:kv], "rp", "w2loc", near)
+    g.wait_ge(sem["cpA1"], 4 - VIA)
+    send(dst["A"], T.lA[:, kv:512], T.pA[:, kv:512], "inA1", "ploc", far)
     g.wait_ge(sem["qtB"], 1)
     send(dst["B"], u8("rtq", 0, NC), u8("tqB", 0, NC), "rt", "ploc", far)
     send(dst["B"], T.rts[:, :], T.tsB[:, :], "rt", "ploc", far)
@@ -137,7 +145,7 @@ def rank_program(g, core, T, topo):
     send(dst["S"], T.lS[:, SPLIT:512], T.pS[:, SPLIT:512], "inS1", "ploc", far)
     g.wait_ge(sem["qh"], 1)
     bcast("h", "hloc")
-    g.wait_ge(sem["w2loc"], 3 * bits(near))
+    g.wait_ge(sem["w2loc"], 3 * bits(near) + nf)
 
     def mm(bank, w, wi, xq, xs, start, stop, done=None):
         c = te.matmul_mx(T.ps[:, 512 * bank:512 * bank + NC], T[w + "q"][:, NC * wi:NC * wi + NC], T[w + "s"][:, NC * wi:NC * wi + NC],
@@ -161,7 +169,8 @@ def rank_program(g, core, T, topo):
     te.wait_ge(sem["x%d" % rel["B"]], 2 * nf)
     four(4, "w1", "xqB", "xsB", "zB")
     te.wait_ge(sem["x%d" % rel["S"]], 2 * nf)
-    te.wait_ge(sem["cpA"], 4)
+    te.wait_ge(sem["cpA0"], VIA)
+    te.wait_ge(sem["cpA1"], 4 - VIA)
     four(0, "w1", "xqS", "xsS", "zS")
     te.wait_ge(sem["qtB"], 1)
     te.wait_ge(sem["qtS"], 1)
@@ -191,6 +200,14 @@ def rank_program(g, core, T, topo):
     def psb(base, b):
         return T.ps[:, 512 * (base + b):512 * (base + b) + NC]
 
+    def copy(out, base, b, ready, dv, ds):
+        if b % 2 == 0:
+            ve.wait_ge(sem[ready], 1)
+            ve.tensor_copy(out, psb(base, b)).then_inc(sem[dv], 1)
+        else:
+            sc.wait_ge(sem[ready], 1)
+            sc.activation(out, psb(base, b), ActivationFunctionType.Copy).then_inc(sem[ds], 1)
+
     def act(p, base):
         for b in range(4):
             if b % 2 == 0:
@@ -202,33 +219,27 @@ def rank_program(g, core, T, topo):
         ve.wait_ge(sem["t" + p], 4)
         ve.quantize_mx(T["tq" + p][:, :], T["ts" + p][:, :], T["t" + p][:, :]).then_inc(sem["qt" + p], 1)
 
-    def copy_out(p, base):
+    def copy_out(p, base, first):
         for b in range(4):
-            done = "cpA" if p == "A" else ("cpS0" if NC * b < SPLIT else "cpS1")
-            o = T["p" + p][:, NC * b:NC * b + NC]
-            if b % 2 == 0:
-                ve.wait_ge(sem["u%s%d" % (p, b)], 1)
-                ve.tensor_copy(o, psb(base, b)).then_inc(sem[done], 1)
-            else:
-                sc.wait_ge(sem["u%s%d" % (p, b)], 1)
-                sc.activation(o, psb(base, b), ActivationFunctionType.Copy).then_inc(sem[done], 1)
+            done = "cp%s%d" % (p, 0 if b < first else 1)
+            copy(T["p" + p][:, NC * b:NC * b + NC], base, b, "u%s%d" % (p, b), done, done)
 
-    ve.wait_ge(sem["lx"], 16)
-    ve.quantize_mx(T.xqO[:, :], T.xsO[:, :], T.xb[:, :]).then_inc(sem["qx"], 1)
-    ve.wait_ge(sem["lw2"], 16)
-    ve.quantize_mx(T.w2q[:, :], T.w2s[:, :], T.w2b[:, :]).then_inc(sem["qw2"], 1)
-    ve.wait_ge(sem["lw1"], 16)
-    ve.quantize_mx(T.w1q[:, :], T.w1s[:, :], T.w1b[:, :]).then_inc(sem["qw1"], 1)
+    def quant(load, done, q, s, b):
+        ve.wait_ge(sem[load], 16)
+        ve.quantize_mx(T[q][:, :], T[s][:, :], T[b][:, :]).then_inc(sem[done], 1)
+
+    quant("lx", "qx", "xqO", "xsO", "xb")
+    quant("lw1", "qw1", "w1q", "w1s", "w1b")
     act("O", 0)
+    quant("lw2", "qw2", "w2q", "w2s", "w2b")
     act("A", 4)
-    copy_out("A", 0)
+    copy_out("A", 0, VIA)
     act("B", 4)
     act("S", 0)
-    copy_out("S", 4)
-    ve.wait_ge(sem["lw3"], 16)
-    ve.quantize_mx(T.w3q[:, :], T.w3s[:, :], T.w3b[:, :]).then_inc(sem["qw3"], 1)
+    copy_out("S", 4, SPLIT // NC)
 
-    ve.wait_ge(sem["inA"], nf)
+    ve.wait_ge(sem["inA0"], nf)
+    ve.wait_ge(sem["inA1"], nf)
     for b in range(4):
         ve.wait_ge(sem["uO%d" % b], 1)
         ve.tensor_tensor(T.acc[:, NC * b:NC * b + NC], psb(0, b), T.lA[:, NC * b:NC * b + NC], AluOpType.add).then_inc(sem["acc"], 1)
@@ -242,28 +253,23 @@ def rank_program(g, core, T, topo):
         sc.activation(T.hb[:, b:512:4], T.sm[:, NC * b:NC * b + NC], ActivationFunctionType.Relu, scale=C2).then_inc(sem["th"], 1)
     ve.wait_ge(sem["th"], 4)
     ve.quantize_mx(T.hqO[:, :], T.hsO[:, :], T.hb[:, :]).then_inc(sem["qh"], 1)
+    quant("lw3", "qw3", "w3q", "w3s", "w3b")
 
     for p, base in (("O", 4), ("A", 0), ("B", 4), ("S", 0)):
-        for b in (0, 1):
-            ve.wait_ge(sem["v%s%d" % (p, b)], 1)
-            ve.tensor_copy(T["y" + p][:, NC * b:NC * b + NC], psb(base, b)).then_inc(sem["yv" + p], 1)
-        for b in (2, 3):
-            sc.wait_ge(sem["v%s%d" % (p, b)], 1)
-            sc.activation(T["y" + p][:, NC * b:NC * b + NC], psb(base, b), ActivationFunctionType.Copy).then_inc(sem["ys" + p], 1)
+        for b in range(4):
+            copy(T["y" + p][:, NC * b:NC * b + NC], base, b, "v%s%d" % (p, b), "yv" + p, "ys" + p)
 
-    sy.wait_ge(sem["qtO"], 1)
-    sy.dma_start(T.t[who["O"]], T.tO[:, :]).then_inc(sem["outs"], 16)
     sy.wait_ge(sem["xloc"], 6 * nf)
     sy.wait_ge(sem["ploc"], 5 * nf)
-    for p in "ABS":
+    for p in "OABS":
         sy.wait_ge(sem["qt" + p], 1)
         sy.dma_start(T.t[who[p]], T["t" + p][:, :]).then_inc(sem["outs"], 16)
-    sy.wait_ge(sem["th"], 4)
-    sy.dma_start(T.h[:], T.hb[:, :]).then_inc(sem["outs"], 16)
     for p in "OABS":
         c0 = 512 * who[p]
         sy.wait_ge(sem["yv" + p], 2)
         sy.wait_ge(sem["ys" + p], 2)
         sy.dma_start(T.y[:, c0:c0 + 512], T["y" + p][:, :]).then_inc(sem["outs"], 16)
+        if p == "O":
+            sy.dma_start(T.h[:], T.hb[:, :]).then_inc(sem["outs"], 16)
     sy.wait_ge(sem["hloc"], 6 * nf)
     sy.wait_ge(sem["outs"], 16 * 9)

from concourse.mybir import dt, AluOpType, ActivationFunctionType

U8 = dt.uint8
C1, C2 = 0.019, 0.0095
SIM_CORES = 112
NC = 128
SPLIT = 384
VIA = 2
HALF = 256

_B, _F, _Q, _S8 = "bfloat16", "float32", "float8_e4m3fn_x4", "uint8"
SCRATCH = {"ps": ("psum", [128, 4096], _F)}
SCRATCH["xb"] = ("sbuf", [128, 512], _B)
for _k in ("w1", "w2", "w3"):
    SCRATCH[_k + "b"] = ("sbuf", [128, 2048], _B)
    SCRATCH[_k + "q"] = ("sbuf", [128, 512], _Q)
    SCRATCH[_k + "s"] = ("sbuf", [128, 512], _S8)
SCRATCH["rw2q"] = ("sbuf", [128, 512], _Q)
SCRATCH["rw2s"] = ("sbuf", [128, 512], _S8)
for _k in ("x", "h"):
    for _p in ("O", "A", "B", "S"):
        SCRATCH[_k + "q" + _p] = ("sbuf", [128, NC], _Q)
        SCRATCH[_k + "s" + _p] = ("sbuf", [128, NC], _S8)
for _p in ("O", "A", "B", "S"):
    SCRATCH["t" + _p] = ("sbuf", [128, 512], _B)
    SCRATCH["tq" + _p] = ("sbuf", [128, NC], _Q)
    SCRATCH["ts" + _p] = ("sbuf", [128, NC], _S8)
    SCRATCH["y" + _p] = ("sbuf", [128, 512], _F)
SCRATCH["rtq"] = ("sbuf", [128, NC], _Q)
SCRATCH["rts"] = ("sbuf", [128, NC], _S8)
for _k in ("pA", "pS", "lA", "lS", "acc", "sm"):
    SCRATCH[_k] = ("sbuf", [128, 512], _F)
SCRATCH["rp"] = ("sbuf", [128, NC * VIA], _F)
SCRATCH["hb"] = ("sbuf", [128, 512], _B)

SEMAPHORES = ["lx", "lw1", "lw2", "lw3", "qx", "qw1", "qw2", "qw3", "xloc", "w2loc", "ploc", "hloc", "outs",
              "w2p", "w2c", "rp", "rw2", "rt", "inA0", "inA1", "inS0", "inS1", "cpA0", "cpA1", "cpS0", "cpS1",
              "acc", "th", "qh", "fwd"]
SEMAPHORES += ["%s%d" % (_k, _r) for _k in "xh" for _r in range(4)]
SEMAPHORES += ["t" + _p for _p in "OABS"] + ["qt" + _p for _p in "OABS"]
SEMAPHORES += ["z%s%d" % (_p, _b) for _p in "OABS" for _b in range(4)]
SEMAPHORES += ["u%s%d" % (_p, _b) for _p in "OAS" for _b in range(4)]
SEMAPHORES += ["v%s%d" % (_p, _b) for _p in "OABS" for _b in range(4)]
SEMAPHORES += ["yv" + _p for _p in "OABS"] + ["ys" + _p for _p in "OABS"]
SEMAPHORES += ["sm%d" % _b for _b in range(4)]


def relations(T, topo, r):
    n = len(T.cores)
    ch = [topo.chip(c) for c in T.cores]
    planes = []
    for i in range(n):
        for p in planes:
            if topo.same_plane(ch[i], ch[p[0]]):
                p.append(i)
                break
        else:
            planes.append([i])
    mine, other = (planes[0], planes[1]) if r in planes[0] else (planes[1], planes[0])
    k = mine.index(r)
    return {"S": mine[1 - k], "B": other[k], "A": other[1 - k]}


def helper_of(T, topo, r):
    me = T.cores[r]
    for c in range(SIM_CORES):
        if topo.chip(c) == topo.chip(me) and topo.die(c) != topo.die(me) and all(topo.may_write(c, d) for d in T.cores):
            return c
    return None


def rank_program(g, core, T, topo):
    sem = T.sem

    def bits(m):
        return bin(m).count("1")

    def send(dst, out, in_, rsem, lsem, mask):
        rid, pid, _ = topo.addr(dst)
        g.remote_dma(out, in_, sem[rsem], sem[lsem], pid, rid, mask)

    def u8(name, a, b):
        return T[name][:, a:b].bitcast(U8)

    def masks(r):
        far = topo.mask(T.cores[r], T.cores[relations(T, topo, r)["A"]])
        return far, topo.mask(T.cores[r], helper_of(T, topo, r)) & ~far

    kv = NC * VIA
    rank = T.rank_of(core)
    if rank is None:
        for r in range(len(T.cores)):
            if helper_of(T, topo, r) == core:
                rel = relations(T, topo, r)
                to_a, to_b = T.cores[rel["A"]], T.cores[rel["B"]]
                m = topo.mask(core, to_b)
                nn = bits(masks(r)[1])
                g.wait_ge(sem["w2p"], nn)
                send(to_b, T.rw2s[:, :], T.rw2s[:, :], "rw2", "fwd", m)
                g.wait_ge(sem["w2c"], nn)
                send(to_b, u8("rw2q", 0, HALF), u8("rw2q", 0, HALF), "rw2", "fwd", m)
                g.wait_ge(sem["rp"], nn)
                send(to_a, T.lA[:, 0:kv], T.rp[:, :], "inA0", "fwd", m)
                g.wait_ge(sem["fwd"], 3 * bits(m))
        return

    rel = relations(T, topo, rank)
    who = dict(rel)
    who["O"] = rank
    dst = {p: T.cores[rel[p]] for p in "ABS"}
    hlp = helper_of(T, topo, rank)
    far, near = masks(rank)
    nf = bits(far)
    te, ve, sc, sy = g.tensor, g.vector, g.scalar, g.sync

    sy.dma_start(T.xb[:], T.x[:]).then_inc(sem["lx"], 16)
    sy.dma_start(T.w1b[:], T.w1[:]).then_inc(sem["lw1"], 16)
    sy.wait_ge(sem["lx"], 16)
    sy.dma_start(T.w2b[:], T.w2[:]).then_inc(sem["lw2"], 16)
    sy.wait_ge(sem["qtA"], 1)
    sy.dma_start(T.w3b[:], T.w3[:]).then_inc(sem["lw3"], 16)

    def bcast(kind, lsem):
        rsem = "%s%d" % (kind, rank)
        for p in "ABS":
            send(dst[p], T[kind + "s" + p][:, :], T[kind + "sO"][:, :], rsem, lsem, far)
            send(dst[p], u8(kind + "q" + p, 0, NC), u8(kind + "qO", 0, NC), rsem, lsem, far)

    g.wait_ge(sem["qx"], 1)
    bcast("x", "xloc")
    g.wait_ge(sem["qw2"], 1)
    send(hlp, T.rw2s[:, :], T.w2s[:, :], "w2p", "w2loc", near)
    send(hlp, u8("rw2q", 0, HALF), u8("w2q", 0, HALF), "w2c", "w2loc", near)
    send(dst["B"], u8("rw2q", HALF, 512), u8("w2q", HALF, 512), "rw2", "w2loc", far)
    g.wait_ge(sem["cpA0"], VIA)
    send(hlp, T.rp[:, :], T.pA[:, 0:kv], "rp", "w2loc", near)
    g.wait_ge(sem["cpA1"], 4 - VIA)
    send(dst["A"], T.lA[:, kv:512], T.pA[:, kv:512], "inA1", "ploc", far)
    g.wait_ge(sem["qtB"], 1)
    send(dst["B"], u8("rtq", 0, NC), u8("tqB", 0, NC), "rt", "ploc", far)
    send(dst["B"], T.rts[:, :], T.tsB[:, :], "rt", "ploc", far)
    g.wait_ge(sem["cpS0"], 3)
    send(dst["S"], T.lS[:, 0:SPLIT], T.pS[:, 0:SPLIT], "inS0", "ploc", far)
    g.wait_ge(sem["cpS1"], 1)
    send(dst["S"], T.lS[:, SPLIT:512], T.pS[:, SPLIT:512], "inS1", "ploc", far)
    g.wait_ge(sem["qh"], 1)
    bcast("h", "hloc")
    g.wait_ge(sem["w2loc"], 3 * bits(near) + nf)

    def mm(bank, w, wi, xq, xs, start, stop, done=None):
        c = te.matmul_mx(T.ps[:, 512 * bank:512 * bank + NC], T[w + "q"][:, NC * wi:NC * wi + NC], T[w + "s"][:, NC * wi:NC * wi + NC],
                         T[xq][:, :], T[xs][:, :], start, stop)
        if done is not None:
            c.then_inc(sem[done], 1)

    def four(base, w, xq, xs, name):
        for b in range(4):
            mm(base + b, w, b, xq, xs, True, True, "%s%d" % (name, b))

    te.wait_ge(sem["qx"], 1)
    te.wait_ge(sem["qw1"], 1)
    four(0, "w1", "xqO", "xsO", "zO")
    te.wait_ge(sem["x%d" % rel["A"]], 2 * nf)
    four(4, "w1", "xqA", "xsA", "zA")
    te.wait_ge(sem["qw2"], 1)
    te.wait_ge(sem["qtO"], 1)
    te.wait_ge(sem["qtA"], 1)
    four(0, "w2", "tqA", "tsA", "uA")
    te.wait_ge(sem["x%d" % rel["B"]], 2 * nf)
    four(4, "w1", "xqB", "xsB", "zB")
    te.wait_ge(sem["x%d" % rel["S"]], 2 * nf)
    te.wait_ge(sem["cpA0"], VIA)
    te.wait_ge(sem["cpA1"], 4 - VIA)
    four(0, "w1", "xqS", "xsS", "zS")
    te.wait_ge(sem["qtB"], 1)
    te.wait_ge(sem["qtS"], 1)
    four(4, "w2", "tqS", "tsS", "uS")
    for b in range(4):
        mm(b, "w2", b, "tqO", "tsO", True, False)
    te.wait_ge(sem["rw2"], 3 * nf)
    te.wait_ge(sem["rt"], 2 * nf)
    for b in range(4):
        mm(b, "rw2", b, "rtq", "rts", False, True, "uO%d" % b)
    te.wait_ge(sem["qw3"], 1)
    te.wait_ge(sem["cpS0"], 3)
    te.wait_ge(sem["cpS1"], 1)
    te.wait_ge(sem["qh"], 1)
    four(4, "w3", "hqO", "hsO", "vO")
    te.wait_ge(sem["h%d" % rel["A"]], 2 * nf)
    four(0, "w3", "hqA", "hsA", "vA")
    te.wait_ge(sem["h%d" % rel["B"]], 2 * nf)
    te.wait_ge(sem["yvO"], 2)
    te.wait_ge(sem["ysO"], 2)
    four(4, "w3", "hqB", "hsB", "vB")
    te.wait_ge(sem["h%d" % rel["S"]], 2 * nf)
    te.wait_ge(sem["yvA"], 2)
    te.wait_ge(sem["ysA"], 2)
    four(0, "w3", "hqS", "hsS", "vS")

    def psb(base, b):
        return T.ps[:, 512 * (base + b):512 * (base + b) + NC]

    def copy(out, base, b, ready, dv, ds):
        if b % 2 == 0:
            ve.wait_ge(sem[ready], 1)
            ve.tensor_copy(out, psb(base, b)).then_inc(sem[dv], 1)
        else:
            sc.wait_ge(sem[ready], 1)
            sc.activation(out, psb(base, b), ActivationFunctionType.Copy).then_inc(sem[ds], 1)

    def act(p, base):
        for b in range(4):
            if b % 2 == 0:
                ve.wait_ge(sem["z%s%d" % (p, b)], 1)
                ve.tensor_scalar(T["t" + p][:, b:512:4], psb(base, b), 0.0, C1, AluOpType.max, AluOpType.mult).then_inc(sem["t" + p], 1)
            else:
                sc.wait_ge(sem["z%s%d" % (p, b)], 1)
                sc.activation(T["t" + p][:, b:512:4], psb(base, b), ActivationFunctionType.Relu, scale=C1).then_inc(sem["t" + p], 1)
        ve.wait_ge(sem["t" + p], 4)
        ve.quantize_mx(T["tq" + p][:, :], T["ts" + p][:, :], T["t" + p][:, :]).then_inc(sem["qt" + p], 1)

    def copy_out(p, base, first):
        for b in range(4):
            done = "cp%s%d" % (p, 0 if b < first else 1)
            copy(T["p" + p][:, NC * b:NC * b + NC], base, b, "u%s%d" % (p, b), done, done)

    def quant(load, done, q, s, b):
        ve.wait_ge(sem[load], 16)
        ve.quantize_mx(T[q][:, :], T[s][:, :], T[b][:, :]).then_inc(sem[done], 1)

    quant("lx", "qx", "xqO", "xsO", "xb")
    quant("lw1", "qw1", "w1q", "w1s", "w1b")
    act("O", 0)
    quant("lw2", "qw2", "w2q", "w2s", "w2b")
    act("A", 4)
    copy_out("A", 0, VIA)
    act("B", 4)
    act("S", 0)
    copy_out("S", 4, SPLIT // NC)

    ve.wait_ge(sem["inA0"], nf)
    ve.wait_ge(sem["inA1"], nf)
    for b in range(4):
        ve.wait_ge(sem["uO%d" % b], 1)
        ve.tensor_tensor(T.acc[:, NC * b:NC * b + NC], psb(0, b), T.lA[:, NC * b:NC * b + NC], AluOpType.add).then_inc(sem["acc"], 1)
    ve.wait_ge(sem["acc"], 4)
    ve.wait_ge(sem["inS0"], nf)
    for b in range(4):
        if NC * b == SPLIT:
            ve.wait_ge(sem["inS1"], nf)
        ve.tensor_tensor(T.sm[:, NC * b:NC * b + NC], T.acc[:, NC * b:NC * b + NC], T.lS[:, NC * b:NC * b + NC], AluOpType.add).then_inc(sem["sm%d" % b], 1)
        sc.wait_ge(sem["sm%d" % b], 1)
        sc.activation(T.hb[:, b:512:4], T.sm[:, NC * b:NC * b + NC], ActivationFunctionType.Relu, scale=C2).then_inc(sem["th"], 1)
    ve.wait_ge(sem["th"], 4)
    ve.quantize_mx(T.hqO[:, :], T.hsO[:, :], T.hb[:, :]).then_inc(sem["qh"], 1)
    quant("lw3", "qw3", "w3q", "w3s", "w3b")

    for p, base in (("O", 4), ("A", 0), ("B", 4), ("S", 0)):
        for b in range(4):
            copy(T["y" + p][:, NC * b:NC * b + NC], base, b, "v%s%d" % (p, b), "yv" + p, "ys" + p)

    sy.wait_ge(sem["xloc"], 6 * nf)
    sy.wait_ge(sem["ploc"], 5 * nf)
    for p in "OABS":
        sy.wait_ge(sem["qt" + p], 1)
        sy.dma_start(T.t[who[p]], T["t" + p][:, :]).then_inc(sem["outs"], 16)
    for p in "OABS":
        c0 = 512 * who[p]
        sy.wait_ge(sem["yv" + p], 2)
        sy.wait_ge(sem["ys" + p], 2)
        sy.dma_start(T.y[:, c0:c0 + 512], T["y" + p][:, :]).then_inc(sem["outs"], 16)
        if p == "O":
            sy.dma_start(T.h[:], T.hb[:, :]).then_inc(sem["outs"], 16)
    sy.wait_ge(sem["hloc"], 6 * nf)
    sy.wait_ge(sem["outs"], 16 * 9)
